import numpy as np
CORES = [19,147,275,403]
N = 4
S, B = 6, 32
def setup_inputs(rng):
    return {"x": rng.standard_normal((N, 128, S * B), dtype=np.float32), "gate": (0.9375 + 0.03125 * rng.standard_normal((N, 128, S * B), dtype=np.float32))}
def setup_inputs_big(rng):
    d = setup_inputs(rng)
    for k in ("x",): d[k] = (d[k].astype(np.float32) * 1048576.0).astype(d[k].dtype)
    return d
def setup_inputs_small(rng):
    d = setup_inputs(rng)
    for k in ("x",): d[k] = (d[k].astype(np.float32) * (1 / 1048576.0)).astype(d[k].dtype)
    return d
def setup_inputs_apart(rng):
    d = setup_inputs(rng)
    f = (10.0 ** rng.permutation(np.linspace(-1.5, 1.5, N))).astype(np.float32).reshape(N, 1, 1)
    for k in ("x",): d[k] = (d[k].astype(np.float32) * f).astype(d[k].dtype)
    return d
def reference(x, gate):
    X, GATE = x.astype(np.float64), gate.astype(np.float64)
    y = np.zeros((N, 128, S * B)); h = np.zeros((128, B))
    for r in range(N):
        for s in range(S):
            h = GATE[r][:, B * s:B * s + B] * h + X[r][:, B * s:B * s + B]
            y[r][:, B * s:B * s + B] = h
    return {"y": y.astype(np.float32)}

@@ -1,0 +1,172 @@
+from concourse.mybir import AluOpType
+
+N, S, B = 4, 6, 32
+
+SCRATCH = {
+    "w": ("sbuf", [128, S + 1, B], "float32"),
+    "gt": ("sbuf", [128, S, B], "float32"),
+    "p": ("sbuf", [128, S, B], "float32"),
+    "m": ("sbuf", [128, S, B], "float32"),
+    "q": ("sbuf", [128, S, B], "float32"),
+    "hb": ("sbuf", [128, B], "float32"),
+    "yb": ("sbuf", [128, S, B], "float32"),
+    "land0": ("sbuf", [128, B], "float32"),
+    "land1": ("sbuf", [128, 2, B], "float32"),
+    "land2": ("sbuf", [128, 2, B], "float32"),
+    "ps": ("psum", [128, 16, B], "float32"),
+}
+SEMAPHORES = ["xl", "gl", "vs", "ready", "ydone", "stored", "sent", "arr0", "arr1", "arr2"]
+
+
+def _routes(cores, topo):
+    n = len(cores)
+    via = {}
+    for j in range(n - 1):
+        direct = [r for r in range(j + 1, n) if topo.may_write(cores[j], cores[r])]
+        for r in range(j + 1, n):
+            if r in direct:
+                via[(j, r)] = j
+            else:
+                via[(j, r)] = [k for k in direct if topo.may_write(cores[k], cores[r])][0]
+    return via
+
+
+def _bits(mask):
+    return bin(mask).count("1")
+
+
+def rank_program(g, core, T, topo):
+    rank = T.rank_of(core)
+    if rank is None:
+        return
+    cores = list(T.cores)
+    n = len(cores)
+    via = _routes(cores, topo)
+    V = g.vector
+    sem = T.sem
+    mult, add = AluOpType.mult, AluOpType.add
+    w, gt, p, ps = T.w, T.gt, T.p, T.ps
+    first, last = rank == 0, rank == n - 1
+
+    g.sync.dma_start(w[:, 0:S, :], T.x[:, :]).then_inc(sem.xl, 16)
+    if first:
+        g.scalar.dma_start(gt[:, 1:S, :], T.gate[:, B:S * B]).then_inc(sem.gl, 16)
+    else:
+        g.scalar.dma_start(gt[:, :, :], T.gate[:, :]).then_inc(sem.gl, 16)
+
+    cnt = {"n": 0, "w": 0}
+
+    def tt(out, a, b, op, own=None):
+        ins = V.tensor_tensor(out, a, b, op)
+        if own is None:
+            ins.then_inc(sem.vs, 1)
+            cnt["n"] += 1
+        else:
+            ins.then_inc(own, 1)
+
+    def step():
+        if cnt["n"] > cnt["w"]:
+            V.wait_ge(sem.vs, cnt["n"])
+            cnt["w"] = cnt["n"]
+
+    V.wait_ge(sem.gl, 16)
+    lo = 3 if first else 1
+    tt(p[:, lo:S:2, :], gt[:, lo:S:2, :], gt[:, lo - 1:S - 1:2, :], mult)
+    V.wait_ge(sem.xl, 16)
+    tt(ps[:, 0:3, :], gt[:, 1:S:2, :], w[:, 0:S - 1:2, :], mult)
+    step()
+    tt(w[:, 1:S:2, :], ps[:, 0:3, :], w[:, 1:S:2, :], add)
+    step()
+    tt(ps[:, 3, :], p[:, 3, :], w[:, 1, :], mult)
+    step()
+    tt(w[:, 3, :], ps[:, 3, :], w[:, 3, :], add)
+    if not first:
+        tt(p[:, 3, :], p[:, 3, :], p[:, 1, :], mult)
+    step()
+    tt(ps[:, 4, :], p[:, 5, :], w[:, 3, :], mult)
+    if not first:
+        tt(w[:, S, :], p[:, 5, :], p[:, 3, :], mult)
+    step()
+    tt(w[:, 5, :], ps[:, 4, :], w[:, 5, :], add, own=sem.ready)
+
+    sent = [0]
+
+    def write(dst_rank, j, src):
+        d = cores[dst_rank]
+        rid, pid = topo.addr(d, core)
+        mk = topo.mask(core, d)
+        land = T["land%d" % j]
+        g.remote_dma(out_ap=land[:] if j == 0 else land[:, :, :], in_ap=src, remote_sem=sem["arr%d" % j],
+                     local_sem=sem.sent, pid=pid, routing_id=rid, dma_engine_mask=mk)
+        sent[0] += _bits(mk)
+
+    def arrival(j):
+        return _bits(topo.mask(cores[via[(j, rank)]], core))
+
+    relays = [(j, r) for (j, r) in sorted(via) if via[(j, r)] == rank and j != rank]
+    if not last:
+        g.wait_ge(sem.ready, 1)
+        own = [r for r in range(rank + 1, n) if via[(rank, r)] == rank]
+        passes_on = [r for r in own if r in [via[k] for k in via if k[0] == rank]]
+        for r in passes_on + [r for r in own if r not in passes_on]:
+            write(r, rank, w[:, 5, :] if first else w[:, 5:S + 1, :])
+    for (j, r) in relays:
+        g.wait_ge(sem["arr%d" % j], arrival(j))
+        write(r, j, T.land0[:] if j == 0 else T["land%d" % j][:, :, :])
+    if sent[0]:
+        g.wait_ge(sem.sent, sent[0])
+
+    tt(ps[:, 5:7, :], gt[:, 2:S - 1:2, :], w[:, 1:S - 2:2, :], mult)
+    if not first:
+        tt(p[:, 2:S - 1:2, :], gt[:, 2:S - 1:2, :], p[:, 1:S - 2:2, :], mult)
+    step()
+    V.wait_ge(sem.ready, 1)
+    if first:
+        tt(w[:, 2:S - 1:2, :], ps[:, 5:7, :], w[:, 2:S - 1:2, :], add, own=sem.ydone)
+        g.sync.wait_ge(sem.ydone, 1)
+        g.sync.dma_start(T.y[:, :], w[:, 0:S, :]).then_inc(sem.stored, 16)
+        g.sync.wait_ge(sem.stored, 16)
+        return
+    tt(w[:, 2:S - 1:2, :], ps[:, 5:7, :], w[:, 2:S - 1:2, :], add)
+    step()
+
+    M = w[:, 0:S, :]
+    Q = [gt[:, 0, :], p[:, 1, :], p[:, 2, :], p[:, 3, :], p[:, 4, :], w[:, S, :]]
+    top = rank - 1
+    late = [j for j in range(rank) if via[(j, rank)] != j]
+    folded = False
+    while top >= 1 and top not in late and [j for j in late if j < top]:
+        land = T["land%d" % top]
+        V.wait_ge(sem["arr%d" % top], arrival(top))
+        for s in range(S):
+            tt(ps[:, 8 + s, :], Q[s], land[:, 0, :], mult)
+        if folded:
+            step()
+        for s in range(S):
+            tt(T.q[:, s, :], Q[s], land[:, 1, :], mult)
+        step()
+        tt(T.m[:, :, :], ps[:, 8:8 + S, :], M, add)
+        step()
+        M = T.m[:, :, :]
+        Q = [T.q[:, s, :] for s in range(S)]
+        folded = True
+        top -= 1
+
+    V.wait_ge(sem.arr0, arrival(0))
+    H = T.land0[:]
+    for j in range(1, top + 1):
+        land = T["land%d" % j]
+        V.wait_ge(sem["arr%d" % j], arrival(j))
+        tt(ps[:, 7, :], land[:, 1, :], H, mult)
+        step()
+        tt(T.hb[:], ps[:, 7, :], land[:, 0, :], add)
+        step()
+        H = T.hb[:]
+
+    for s in range(S):
+        tt(ps[:, 8 + s, :], Q[s], H, mult)
+    step()
+    tt(T.yb[:, :, :], ps[:, 8:8 + S, :], M, add, own=sem.ydone)
+    g.sync.wait_ge(sem.ydone, 1)
+    g.sync.dma_start(T.y[:, :], T.yb[:, :, :]).then_inc(sem.stored, 16)
+    g.sync.wait_ge(sem.stored, 16)

@@ -6,6 +6,7 @@ SCRATCH = {
     "w": ("sbuf", [128, S + 1, B], "float32"),
     "gt": ("sbuf", [128, S, B], "float32"),
     "p": ("sbuf", [128, S, B], "float32"),
+    "pr": ("sbuf", [128, 2, B], "float32"),
     "m": ("sbuf", [128, S, B], "float32"),
     "q": ("sbuf", [128, S, B], "float32"),
     "hb": ("sbuf", [128, B], "float32"),
@@ -15,7 +16,8 @@ SCRATCH = {
     "land2": ("sbuf", [128, 2, B], "float32"),
     "ps": ("psum", [128, 16, B], "float32"),
 }
-SEMAPHORES = ["xl", "gl", "vs", "ready", "ydone", "stored", "sent", "arr0", "arr1", "arr2"]
+SEMAPHORES = ["xl", "gl", "vs", "ready", "ydone", "stored", "sent", "arr0", "arr1", "arr2",
+              "sa1", "st3", "sa2", "sb1", "saa", "spr", "sss", "f1", "f2"]
 
 
 def _routes(cores, topo):
@@ -45,14 +47,14 @@ def rank_program(g, core, T, topo):
     V = g.vector
     sem = T.sem
     mult, add = AluOpType.mult, AluOpType.add
-    w, gt, p, ps = T.w, T.gt, T.p, T.ps
+    w, gt, p, ps, pr = T.w, T.gt, T.p, T.ps, T.pr
     first, last = rank == 0, rank == n - 1
 
-    g.sync.dma_start(w[:, 0:S, :], T.x[:, :]).then_inc(sem.xl, 16)
     if first:
-        g.scalar.dma_start(gt[:, 1:S, :], T.gate[:, B:S * B]).then_inc(sem.gl, 16)
+        g.sync.dma_start(gt[:, 1:S, :], T.gate[:, B:S * B]).then_inc(sem.gl, 16)
     else:
-        g.scalar.dma_start(gt[:, :, :], T.gate[:, :]).then_inc(sem.gl, 16)
+        g.sync.dma_start(gt[:, :, :], T.gate[:, :]).then_inc(sem.gl, 16)
+    g.scalar.dma_start(w[:, 0:S, :], T.x[:, :]).then_inc(sem.xl, 16)
 
     cnt = {"n": 0, "w": 0}
 
@@ -69,25 +71,26 @@ def rank_program(g, core, T, topo):
             V.wait_ge(sem.vs, cnt["n"])
             cnt["w"] = cnt["n"]
 
-    V.wait_ge(sem.gl, 16)
     lo = 3 if first else 1
-    tt(p[:, lo:S:2, :], gt[:, lo:S:2, :], gt[:, lo - 1:S - 1:2, :], mult)
+    V.wait_ge(sem.gl, 16)
+    tt(p[:, lo:S:2, :], gt[:, lo:S:2, :], gt[:, lo - 1:S - 1:2, :], mult, own=sem.sa1)
     V.wait_ge(sem.xl, 16)
-    tt(ps[:, 0:3, :], gt[:, 1:S:2, :], w[:, 0:S - 1:2, :], mult)
-    step()
-    tt(w[:, 1:S:2, :], ps[:, 0:3, :], w[:, 1:S:2, :], add)
-    step()
-    tt(ps[:, 3, :], p[:, 3, :], w[:, 1, :], mult)
-    step()
-    tt(w[:, 3, :], ps[:, 3, :], w[:, 3, :], add)
+    tt(ps[:, 0:3, :], gt[:, 1:S:2, :], w[:, 0:S - 1:2, :], mult, own=sem.st3)
+    V.wait_ge(sem.sa1, 1)
+    tt(p[:, 4, :], p[:, 5, :], p[:, 3, :], mult, own=sem.sa2)
+    V.wait_ge(sem.st3, 1)
+    tt(w[:, 1:S:2, :], ps[:, 0:3, :], w[:, 1:S:2, :], add, own=sem.sb1)
+    V.wait_ge(sem.sa2, 1)
     if not first:
-        tt(p[:, 3, :], p[:, 3, :], p[:, 1, :], mult)
-    step()
-    tt(ps[:, 4, :], p[:, 5, :], w[:, 3, :], mult)
+        tt(w[:, S, :], p[:, 4, :], p[:, 1, :], mult, own=sem.saa)
+    V.wait_ge(sem.sb1, 1)
+    tt(pr[:, :, :], p[:, 4:6, :], w[:, 1:4:2, :], mult, own=sem.spr)
+    V.wait_ge(sem.spr, 1)
+    tt(ps[:, 3, :], pr[:, 0, :], pr[:, 1, :], add, own=sem.sss)
+    V.wait_ge(sem.sss, 1)
     if not first:
-        tt(w[:, S, :], p[:, 5, :], p[:, 3, :], mult)
-    step()
-    tt(w[:, 5, :], ps[:, 4, :], w[:, 5, :], add, own=sem.ready)
+        V.wait_ge(sem.saa, 1)
+    tt(w[:, 5, :], ps[:, 3, :], w[:, 5, :], add, own=sem.ready)
 
     sent = [0]
 
@@ -116,22 +119,28 @@ def rank_program(g, core, T, topo):
     if sent[0]:
         g.wait_ge(sem.sent, sent[0])
 
+    tt(ps[:, 4, :], p[:, 3, :], w[:, 1, :], mult)
+    step()
+    tt(w[:, 3, :], ps[:, 4, :], w[:, 3, :], add)
+    if not first:
+        tt(p[:, 3, :], p[:, 3, :], p[:, 1, :], mult)
+    step()
     tt(ps[:, 5:7, :], gt[:, 2:S - 1:2, :], w[:, 1:S - 2:2, :], mult)
     if not first:
         tt(p[:, 2:S - 1:2, :], gt[:, 2:S - 1:2, :], p[:, 1:S - 2:2, :], mult)
     step()
-    V.wait_ge(sem.ready, 1)
+    tt(w[:, 2:S - 1:2, :], ps[:, 5:7, :], w[:, 2:S - 1:2, :], add)
+    step()
     if first:
-        tt(w[:, 2:S - 1:2, :], ps[:, 5:7, :], w[:, 2:S - 1:2, :], add, own=sem.ydone)
-        g.sync.wait_ge(sem.ydone, 1)
+        g.sync.wait_ge(sem.vs, cnt["n"])
+        g.sync.wait_ge(sem.ready, 1)
         g.sync.dma_start(T.y[:, :], w[:, 0:S, :]).then_inc(sem.stored, 16)
         g.sync.wait_ge(sem.stored, 16)
         return
-    tt(w[:, 2:S - 1:2, :], ps[:, 5:7, :], w[:, 2:S - 1:2, :], add)
-    step()
+    V.wait_ge(sem.ready, 1)
 
-    M = w[:, 0:S, :]
-    Q = [gt[:, 0, :], p[:, 1, :], p[:, 2, :], p[:, 3, :], p[:, 4, :], w[:, S, :]]
+    M = w
+    Q = [gt[:, 0, :]] + [p[:, s, :] for s in range(1, S - 1)] + [w[:, S, :]]
     top = rank - 1
     late = [j for j in range(rank) if via[(j, rank)] != j]
     folded = False
@@ -145,9 +154,9 @@ def rank_program(g, core, T, topo):
         for s in range(S):
             tt(T.q[:, s, :], Q[s], land[:, 1, :], mult)
         step()
-        tt(T.m[:, :, :], ps[:, 8:8 + S, :], M, add)
+        tt(T.m[:, :, :], ps[:, 8:8 + S, :], M[:, 0:S, :], add)
         step()
-        M = T.m[:, :, :]
+        M = T.m
         Q = [T.q[:, s, :] for s in range(S)]
         folded = True
         top -= 1
@@ -163,10 +172,13 @@ def rank_program(g, core, T, topo):
         step()
         H = T.hb[:]
 
+    h = S // 2
     for s in range(S):
-        tt(ps[:, 8 + s, :], Q[s], H, mult)
-    step()
-    tt(T.yb[:, :, :], ps[:, 8:8 + S, :], M, add, own=sem.ydone)
-    g.sync.wait_ge(sem.ydone, 1)
+        tt(ps[:, 8 + s, :], Q[s], H, mult, own=sem.f1 if s < h else sem.f2)
+    V.wait_ge(sem.f1, h)
+    tt(T.yb[:, 0:h, :], ps[:, 8:8 + h, :], M[:, 0:h, :], add, own=sem.ydone)
+    V.wait_ge(sem.f2, S - h)
+    tt(T.yb[:, h:S, :], ps[:, 8 + h:8 + S, :], M[:, h:S, :], add, own=sem.ydone)
+    g.sync.wait_ge(sem.ydone, 2)
     g.sync.dma_start(T.y[:, :], T.yb[:, :, :]).then_inc(sem.stored, 16)
     g.sync.wait_ge(sem.stored, 16)

@@ -8,21 +8,23 @@ SCRATCH = {
     "p": ("sbuf", [128, S, B], "float32"),
     "pr": ("sbuf", [128, 2, B], "float32"),
     "m": ("sbuf", [128, S, B], "float32"),
-    "q": ("sbuf", [128, S, B], "float32"),
-    "hb": ("sbuf", [128, B], "float32"),
+    "hb": ("sbuf", [128, 2, B], "float32"),
+    "zb": ("sbuf", [128, B], "float32"),
     "yb": ("sbuf", [128, S, B], "float32"),
     "land0": ("sbuf", [128, B], "float32"),
+    "landa": ("sbuf", [128, B], "float32"),
     "land1": ("sbuf", [128, 2, B], "float32"),
     "land2": ("sbuf", [128, 2, B], "float32"),
     "ps": ("psum", [128, 16, B], "float32"),
+    "pq": ("psum", [128, S, B], "float32"),
 }
-SEMAPHORES = ["xl", "gl", "vs", "ready", "ydone", "stored", "sent", "arr0", "arr1", "arr2",
-              "sa1", "st3", "sa2", "sb1", "saa", "spr", "sss", "f1", "f2"]
+SEMAPHORES = ["xl", "gl", "vs", "ready", "ydone", "stored", "sent", "arr0", "arr1", "arr2", "arra",
+              "sa1", "st3", "sa2", "sb1", "saa", "spr", "sp1", "sss", "f1", "f2", "sz"]
 
 
 def _routes(cores, topo):
     n = len(cores)
-    via = {}
+    via, mul = {}, {}
     for j in range(n - 1):
         direct = [r for r in range(j + 1, n) if topo.may_write(cores[j], cores[r])]
         for r in range(j + 1, n):
@@ -30,7 +32,9 @@ def _routes(cores, topo):
                 via[(j, r)] = j
             else:
                 via[(j, r)] = [k for k in direct if topo.may_write(cores[k], cores[r])][0]
-    return via
+                if j == 1 and topo.may_write(cores[j], cores[0]) and topo.may_write(cores[0], cores[r]):
+                    mul[(j, r)] = 0
+    return via, mul
 
 
 def _bits(mask):
@@ -43,7 +47,7 @@ def rank_program(g, core, T, topo):
         return
     cores = list(T.cores)
     n = len(cores)
-    via = _routes(cores, topo)
+    via, mul = _routes(cores, topo)
     V = g.vector
     sem = T.sem
     mult, add = AluOpType.mult, AluOpType.add
@@ -84,38 +88,54 @@ def rank_program(g, core, T, topo):
     if not first:
         tt(w[:, S, :], p[:, 4, :], p[:, 1, :], mult, own=sem.saa)
     V.wait_ge(sem.sb1, 1)
-    tt(pr[:, :, :], p[:, 4:6, :], w[:, 1:4:2, :], mult, own=sem.spr)
+    tt(pr[:, 1, :], p[:, 5, :], w[:, 3, :], mult, own=sem.spr)
+    tt(pr[:, 0, :], p[:, 4, :], w[:, 1, :], mult, own=sem.sp1)
     V.wait_ge(sem.spr, 1)
-    tt(ps[:, 3, :], pr[:, 0, :], pr[:, 1, :], add, own=sem.sss)
+    tt(ps[:, 3, :], pr[:, 1, :], w[:, 5, :], add, own=sem.sss)
     V.wait_ge(sem.sss, 1)
+    V.wait_ge(sem.sp1, 1)
     if not first:
         V.wait_ge(sem.saa, 1)
-    tt(w[:, 5, :], ps[:, 3, :], w[:, 5, :], add, own=sem.ready)
+    tt(w[:, 5, :], ps[:, 3, :], pr[:, 0, :], add, own=sem.ready)
 
     sent = [0]
 
-    def write(dst_rank, j, src):
+    def write(dst_rank, out, src, rsem):
         d = cores[dst_rank]
         rid, pid = topo.addr(d, core)
         mk = topo.mask(core, d)
-        land = T["land%d" % j]
-        g.remote_dma(out_ap=land[:] if j == 0 else land[:, :, :], in_ap=src, remote_sem=sem["arr%d" % j],
-                     local_sem=sem.sent, pid=pid, routing_id=rid, dma_engine_mask=mk)
+        g.remote_dma(out_ap=out, in_ap=src, remote_sem=rsem, local_sem=sem.sent, pid=pid, routing_id=rid,
+                     dma_engine_mask=mk)
         sent[0] += _bits(mk)
 
-    def arrival(j):
-        return _bits(topo.mask(cores[via[(j, rank)]], core))
+    def count(src_rank):
+        return _bits(topo.mask(cores[src_rank], core))
 
-    relays = [(j, r) for (j, r) in sorted(via) if via[(j, r)] == rank and j != rank]
+    for (j, r) in sorted(mul):
+        if j == rank:
+            g.wait_ge(sem.saa, 1)
+            write(mul[(j, r)], T.landa[:], w[:, S, :], sem.arra)
     if not last:
         g.wait_ge(sem.ready, 1)
         own = [r for r in range(rank + 1, n) if via[(rank, r)] == rank]
+        own = [r for r in own if not [k for k in mul if k[1] == r and mul[k] == rank]]
         passes_on = [r for r in own if r in [via[k] for k in via if k[0] == rank]]
         for r in passes_on + [r for r in own if r not in passes_on]:
-            write(r, rank, w[:, 5, :] if first else w[:, 5:S + 1, :])
-    for (j, r) in relays:
-        g.wait_ge(sem["arr%d" % j], arrival(j))
-        write(r, j, T.land0[:] if j == 0 else T["land%d" % j][:, :, :])
+            if first:
+                write(r, T.land0[:], w[:, 5, :], sem.arr0)
+            else:
+                write(r, T["land%d" % rank][:, :, :], w[:, 5:S + 1, :], sem["arr%d" % rank])
+    for (j, r) in sorted(via):
+        if via[(j, r)] == rank and j != rank:
+            g.wait_ge(sem["arr%d" % j], count(j))
+            if j == 0:
+                write(r, T.land0[:], T.land0[:], sem.arr0)
+            else:
+                write(r, T["land%d" % j][:, 0, :], T["land%d" % j][:, 0, :], sem["arr%d" % j])
+    for (j, r) in sorted(mul):
+        if mul[(j, r)] == rank:
+            g.wait_ge(sem.sz, 1)
+            write(r, T.land0[:], T.zb[:], sem.arr0)
     if sent[0]:
         g.wait_ge(sem.sent, sent[0])
 
@@ -131,53 +151,54 @@ def rank_program(g, core, T, topo):
     step()
     tt(w[:, 2:S - 1:2, :], ps[:, 5:7, :], w[:, 2:S - 1:2, :], add)
     step()
+    V.wait_ge(sem.ready, 1)
     if first:
         g.sync.wait_ge(sem.vs, cnt["n"])
         g.sync.wait_ge(sem.ready, 1)
         g.sync.dma_start(T.y[:, :], w[:, 0:S, :]).then_inc(sem.stored, 16)
         g.sync.wait_ge(sem.stored, 16)
+        for (j, r) in sorted(mul):
+            if mul[(j, r)] == rank:
+                V.wait_ge(sem.arra, count(j))
+                tt(T.zb[:], T.landa[:], w[:, 5, :], mult, own=sem.sz)
         return
-    V.wait_ge(sem.ready, 1)
 
     M = w
     Q = [gt[:, 0, :]] + [p[:, s, :] for s in range(1, S - 1)] + [w[:, S, :]]
     top = rank - 1
-    late = [j for j in range(rank) if via[(j, rank)] != j]
-    folded = False
-    while top >= 1 and top not in late and [j for j in late if j < top]:
+    if top >= 1:
         land = T["land%d" % top]
-        V.wait_ge(sem["arr%d" % top], arrival(top))
+        V.wait_ge(sem["arr%d" % top], count(top))
         for s in range(S):
             tt(ps[:, 8 + s, :], Q[s], land[:, 0, :], mult)
-        if folded:
-            step()
         for s in range(S):
-            tt(T.q[:, s, :], Q[s], land[:, 1, :], mult)
+            tt(T.pq[:, s, :], Q[s], land[:, 1, :], mult)
         step()
-        tt(T.m[:, :, :], ps[:, 8:8 + S, :], M[:, 0:S, :], add)
+        tt(T.m[:, :, :], ps[:, 8:8 + S, :], w[:, 0:S, :], add)
         step()
         M = T.m
-        Q = [T.q[:, s, :] for s in range(S)]
-        folded = True
+        Q = [T.pq[:, s, :] for s in range(S)]
         top -= 1
 
-    V.wait_ge(sem.arr0, arrival(0))
-    H = T.land0[:]
-    for j in range(1, top + 1):
-        land = T["land%d" % j]
-        V.wait_ge(sem["arr%d" % j], arrival(j))
-        tt(ps[:, 7, :], land[:, 1, :], H, mult)
-        step()
-        tt(T.hb[:], ps[:, 7, :], land[:, 0, :], add)
-        step()
-        H = T.hb[:]
-
-    h = S // 2
-    for s in range(S):
-        tt(ps[:, 8 + s, :], Q[s], H, mult, own=sem.f1 if s < h else sem.f2)
-    V.wait_ge(sem.f1, h)
+    V.wait_ge(sem.arr0, count(via[(0, rank)]))
+    if top == 0:
+        h = S // 2
+        for s in range(S):
+            tt(ps[:, 8 + s, :], Q[s], T.land0[:], mult, own=sem.f1 if s < h else sem.f2)
+        V.wait_ge(sem.f1, h)
+        nf2 = S - h
+    else:
+        V.wait_ge(sem.arr1, count(via[(1, rank)]))
+        tt(T.hb[:, 0, :], T.land0[:], T.land1[:, 0, :], add, own=sem.sz)
+        tt(T.hb[:, 1, :], T.land0[:], T.land1[:, 0, :], add, own=sem.sz)
+        V.wait_ge(sem.sz, 2)
+        h = 4
+        for s in range(0, S, 2):
+            tt(ps[:, 8 + s:10 + s, :], T.pq[:, s:s + 2, :], T.hb[:, :, :], mult, own=sem.f1 if s < h else sem.f2)
+        V.wait_ge(sem.f1, h // 2)
+        nf2 = (S - h) // 2
     tt(T.yb[:, 0:h, :], ps[:, 8:8 + h, :], M[:, 0:h, :], add, own=sem.ydone)
-    V.wait_ge(sem.f2, S - h)
+    V.wait_ge(sem.f2, nf2)
     tt(T.yb[:, h:S, :], ps[:, 8 + h:8 + S, :], M[:, h:S, :], add, own=sem.ydone)
     g.sync.wait_ge(sem.ydone, 2)
     g.sync.dma_start(T.y[:, :], T.yb[:, :, :]).then_inc(sem.stored, 16)

@@ -7,34 +7,47 @@ SCRATCH = {
     "gt": ("sbuf", [128, S, B], "float32"),
     "p": ("sbuf", [128, S, B], "float32"),
     "pr": ("sbuf", [128, 2, B], "float32"),
+    "c2b": ("sbuf", [128, B], "float32"),
+    "bb": ("sbuf", [128, B], "float32"),
+    "lb": ("sbuf", [128, B], "float32"),
+    "la": ("sbuf", [128, 2, B], "float32"),
+    "ap": ("sbuf", [128, B], "float32"),
+    "a1b": ("sbuf", [128, B], "float32"),
+    "b0": ("sbuf", [128, B], "float32"),
+    "b2": ("sbuf", [128, B], "float32"),
     "m": ("sbuf", [128, S, B], "float32"),
     "hb": ("sbuf", [128, 2, B], "float32"),
     "zb": ("sbuf", [128, B], "float32"),
     "yb": ("sbuf", [128, S, B], "float32"),
-    "land0": ("sbuf", [128, B], "float32"),
+    "land0": ("sbuf", [128, 2, B], "float32"),
     "landa": ("sbuf", [128, B], "float32"),
     "land1": ("sbuf", [128, 2, B], "float32"),
     "land2": ("sbuf", [128, 2, B], "float32"),
+    "lg0": ("sbuf", [128, B], "float32"),
+    "le0": ("sbuf", [128, B], "float32"),
+    "ll0": ("sbuf", [128, B], "float32"),
+    "le2": ("sbuf", [128, B], "float32"),
     "ps": ("psum", [128, 16, B], "float32"),
     "pq": ("psum", [128, S, B], "float32"),
 }
-SEMAPHORES = ["xl", "gl", "vs", "ready", "ydone", "stored", "sent", "arr0", "arr1", "arr2", "arra",
-              "sa1", "st3", "sa2", "sb1", "saa", "spr", "sp1", "sss", "f1", "f2", "sz"]
+SEMAPHORES = ["xl", "gl", "vs", "ready", "ydone", "stored", "sent", "es", "arr0", "arr1", "arr2", "arra", "arrp",
+              "ag0", "ae0", "al0", "ae2", "sa1", "st3", "sa2", "sb1", "saa", "spr", "sp1", "sss", "f1", "f2", "sz",
+              "sc2", "sl1", "lrdy", "sap", "sq"]
 
 
 def _routes(cores, topo):
     n = len(cores)
-    via, mul = {}, {}
-    for j in range(n - 1):
-        direct = [r for r in range(j + 1, n) if topo.may_write(cores[j], cores[r])]
+
+    def ok(a, b):
+        return topo.may_write(cores[a], cores[b])
+
+    way = {}
+    for j in range(n):
         for r in range(j + 1, n):
-            if r in direct:
-                via[(j, r)] = j
-            else:
-                via[(j, r)] = [k for k in direct if topo.may_write(cores[k], cores[r])][0]
-                if j == 1 and topo.may_write(cores[j], cores[0]) and topo.may_write(cores[0], cores[r]):
-                    mul[(j, r)] = 0
-    return via, mul
+            if not ok(j, r):
+                c = [k for k in range(n) if k not in (j, r) and ok(j, k) and ok(k, r)]
+                way[(j, r)] = [k for k in c if j < k < r] + [k for k in c if not j < k < r]
+    return way
 
 
 def _bits(mask):
@@ -47,12 +60,15 @@ def rank_program(g, core, T, topo):
         return
     cores = list(T.cores)
     n = len(cores)
-    via, mul = _routes(cores, topo)
+    way = _routes(cores, topo)
+    assert sorted(way) == [(0, 2), (1, 3)] and way[(0, 2)][0] == 1 and way[(1, 3)] == [2, 0]
     V = g.vector
     sem = T.sem
     mult, add = AluOpType.mult, AluOpType.add
     w, gt, p, ps, pr = T.w, T.gt, T.p, T.ps, T.pr
-    first, last = rank == 0, rank == n - 1
+    first = rank == 0
+    raw5 = rank in (0, 2)
+    A = T.la[:, 1, :] if rank == 2 else w[:, S, :]
 
     if first:
         g.sync.dma_start(gt[:, 1:S, :], T.gate[:, B:S * B]).then_inc(sem.gl, 16)
@@ -83,59 +99,88 @@ def rank_program(g, core, T, topo):
     V.wait_ge(sem.sa1, 1)
     tt(p[:, 4, :], p[:, 5, :], p[:, 3, :], mult, own=sem.sa2)
     V.wait_ge(sem.st3, 1)
-    tt(w[:, 1:S:2, :], ps[:, 0:3, :], w[:, 1:S:2, :], add, own=sem.sb1)
+    if raw5:
+        tt(w[:, 1:4:2, :], ps[:, 0:2, :], w[:, 1:4:2, :], add, own=sem.sb1)
+    else:
+        tt(w[:, 1:S:2, :], ps[:, 0:3, :], w[:, 1:S:2, :], add, own=sem.sb1)
     V.wait_ge(sem.sa2, 1)
-    if not first:
-        tt(w[:, S, :], p[:, 4, :], p[:, 1, :], mult, own=sem.saa)
+    if first:
+        tt(T.c2b[:], ps[:, 2, :], w[:, 5, :], add, own=sem.sc2)
+    else:
+        tt(A, p[:, 4, :], p[:, 1, :], mult, own=sem.saa)
     V.wait_ge(sem.sb1, 1)
     tt(pr[:, 1, :], p[:, 5, :], w[:, 3, :], mult, own=sem.spr)
     tt(pr[:, 0, :], p[:, 4, :], w[:, 1, :], mult, own=sem.sp1)
     V.wait_ge(sem.spr, 1)
-    tt(ps[:, 3, :], pr[:, 1, :], w[:, 5, :], add, own=sem.sss)
-    V.wait_ge(sem.sss, 1)
-    V.wait_ge(sem.sp1, 1)
-    if not first:
+    if first:
+        V.wait_ge(sem.sc2, 1)
+        tt(ps[:, 3, :], pr[:, 1, :], T.c2b[:], add, own=sem.sss)
+        tt(ps[:, 7, :], pr[:, 1, :], ps[:, 2, :], add, own=sem.sl1)
+        V.wait_ge(sem.sss, 1)
+        V.wait_ge(sem.sp1, 1)
+        tt(T.bb[:], ps[:, 3, :], pr[:, 0, :], add, own=sem.ready)
+        V.wait_ge(sem.sl1, 1)
+        tt(T.lb[:], ps[:, 7, :], pr[:, 0, :], add, own=sem.lrdy)
+    elif rank == 2:
+        tt(ps[:, 3, :], pr[:, 1, :], ps[:, 2, :], add, own=sem.sss)
+        V.wait_ge(sem.sss, 1)
+        V.wait_ge(sem.sp1, 1)
         V.wait_ge(sem.saa, 1)
-    tt(w[:, 5, :], ps[:, 3, :], pr[:, 0, :], add, own=sem.ready)
+        tt(T.la[:, 0, :], ps[:, 3, :], pr[:, 0, :], add, own=sem.ready)
+    else:
+        tt(ps[:, 3, :], pr[:, 1, :], w[:, 5, :], add, own=sem.sss)
+        if rank == 1:
+            tt(T.ap[:], p[:, 4, :], gt[:, 1, :], mult, own=sem.sap)
+        V.wait_ge(sem.sss, 1)
+        V.wait_ge(sem.sp1, 1)
+        V.wait_ge(sem.saa, 1)
+        tt(w[:, 5, :], ps[:, 3, :], pr[:, 0, :], add, own=sem.ready)
+        if rank == 1:
+            V.wait_ge(sem.sap, 1)
 
     sent = [0]
 
-    def write(dst_rank, out, src, rsem):
+    def write(dst_rank, out, src, rsem, lsem=None):
         d = cores[dst_rank]
         rid, pid = topo.addr(d, core)
         mk = topo.mask(core, d)
-        g.remote_dma(out_ap=out, in_ap=src, remote_sem=rsem, local_sem=sem.sent, pid=pid, routing_id=rid,
-                     dma_engine_mask=mk)
-        sent[0] += _bits(mk)
+        g.remote_dma(out_ap=out, in_ap=src, remote_sem=rsem, local_sem=sem.sent if lsem is None else lsem, pid=pid,
+                     routing_id=rid, dma_engine_mask=mk)
+        if lsem is None:
+            sent[0] += _bits(mk)
+        return _bits(mk)
 
     def count(src_rank):
         return _bits(topo.mask(cores[src_rank], core))
 
-    for (j, r) in sorted(mul):
-        if j == rank:
-            g.wait_ge(sem.saa, 1)
-            write(mul[(j, r)], T.landa[:], w[:, S, :], sem.arra)
-    if not last:
+    left5 = 0
+    if rank == 0:
+        g.wait_ge(sem.xl, 16)
+        write(3, T.le0[:], w[:, 5, :], sem.ae0)
         g.wait_ge(sem.ready, 1)
-        own = [r for r in range(rank + 1, n) if via[(rank, r)] == rank]
-        own = [r for r in own if not [k for k in mul if k[1] == r and mul[k] == rank]]
-        passes_on = [r for r in own if r in [via[k] for k in via if k[0] == rank]]
-        for r in passes_on + [r for r in own if r not in passes_on]:
-            if first:
-                write(r, T.land0[:], w[:, 5, :], sem.arr0)
-            else:
-                write(r, T["land%d" % rank][:, :, :], w[:, 5:S + 1, :], sem["arr%d" % rank])
-    for (j, r) in sorted(via):
-        if via[(j, r)] == rank and j != rank:
-            g.wait_ge(sem["arr%d" % j], count(j))
-            if j == 0:
-                write(r, T.land0[:], T.land0[:], sem.arr0)
-            else:
-                write(r, T["land%d" % j][:, 0, :], T["land%d" % j][:, 0, :], sem["arr%d" % j])
-    for (j, r) in sorted(mul):
-        if mul[(j, r)] == rank:
-            g.wait_ge(sem.sz, 1)
-            write(r, T.land0[:], T.zb[:], sem.arr0)
+        write(1, T.land0[:, 0, :], T.bb[:], sem.arr0)
+        g.wait_ge(sem.lrdy, 1)
+        write(3, T.ll0[:], T.lb[:], sem.al0)
+        g.wait_ge(sem.arra, count(1))
+        write(3, T.landa[:], T.landa[:], sem.arra)
+    elif rank == 1:
+        g.wait_ge(sem.gl, 16)
+        write(2, T.lg0[:], gt[:, 0, :], sem.ag0)
+        g.wait_ge(sem.saa, 1)
+        write(0, T.landa[:], w[:, S, :], sem.arra)
+        g.wait_ge(sem.ready, 1)
+        write(2, T.land1[:, 0, :], w[:, 5, :], sem.arr1)
+        g.wait_ge(sem.sap, 1)
+        write(2, T.land1[:, 1, :], T.ap[:], sem.arrp)
+        g.wait_ge(sem.arr0, count(0))
+        write(2, T.land0[:, 0, :], T.land0[:, 0, :], sem.arr0)
+    elif rank == 2:
+        g.wait_ge(sem.xl, 16)
+        left5 = write(3, T.le2[:], w[:, 5, :], sem.ae2, lsem=sem.es)
+        g.wait_ge(sem.ready, 1)
+        write(3, T.land2[:, :, :], T.la[:, :, :], sem.arr2)
+        g.wait_ge(sem.arr1, count(1))
+        write(3, T.land1[:, 0, :], T.land1[:, 0, :], sem.arr1)
     if sent[0]:
         g.wait_ge(sem.sent, sent[0])
 
@@ -150,53 +195,80 @@ def rank_program(g, core, T, topo):
         tt(p[:, 2:S - 1:2, :], gt[:, 2:S - 1:2, :], p[:, 1:S - 2:2, :], mult)
     step()
     tt(w[:, 2:S - 1:2, :], ps[:, 5:7, :], w[:, 2:S - 1:2, :], add)
-    step()
     V.wait_ge(sem.ready, 1)
+    if rank == 2:
+        V.wait_ge(sem.es, left5)
+        tt(w[:, 5, :], T.la[:, 0, :], w[:, 5, :], add)
+    step()
     if first:
         g.sync.wait_ge(sem.vs, cnt["n"])
         g.sync.wait_ge(sem.ready, 1)
-        g.sync.dma_start(T.y[:, :], w[:, 0:S, :]).then_inc(sem.stored, 16)
-        g.sync.wait_ge(sem.stored, 16)
-        for (j, r) in sorted(mul):
-            if mul[(j, r)] == rank:
-                V.wait_ge(sem.arra, count(j))
-                tt(T.zb[:], T.landa[:], w[:, 5, :], mult, own=sem.sz)
+        g.sync.dma_start(T.y[:, 0:(S - 1) * B], w[:, 0:S - 1, :]).then_inc(sem.stored, 16)
+        g.sync.dma_start(T.y[:, (S - 1) * B:S * B], T.bb[:]).then_inc(sem.stored, 16)
+        g.sync.wait_ge(sem.stored, 32)
         return
 
     M = w
-    Q = [gt[:, 0, :]] + [p[:, s, :] for s in range(1, S - 1)] + [w[:, S, :]]
-    top = rank - 1
-    if top >= 1:
-        land = T["land%d" % top]
-        V.wait_ge(sem["arr%d" % top], count(top))
+    Q = [gt[:, 0, :]] + [p[:, s, :] for s in range(1, S - 1)] + [A]
+    if rank == 2:
+        V.wait_ge(sem.arr1, count(1))
         for s in range(S):
-            tt(ps[:, 8 + s, :], Q[s], land[:, 0, :], mult)
+            tt(ps[:, 8 + s, :], Q[s], T.land1[:, 0, :], mult)
+        V.wait_ge(sem.ag0, count(1))
+        V.wait_ge(sem.arrp, count(1))
+        tt(T.a1b[:], T.lg0[:], T.land1[:, 1, :], mult, own=sem.sq)
+        step()
+        tt(T.m[:, :, :], ps[:, 8:8 + S, :], w[:, 0:S, :], add)
+        V.wait_ge(sem.sq, 1)
         for s in range(S):
-            tt(T.pq[:, s, :], Q[s], land[:, 1, :], mult)
+            tt(T.pq[:, s, :], Q[s], T.a1b[:], mult)
+        step()
+        M = T.m
+    elif rank == 3:
+        V.wait_ge(sem.ae2, count(2))
+        V.wait_ge(sem.arr2, count(2))
+        tt(T.b2[:], T.le2[:], T.land2[:, 0, :], add, own=sem.sq)
+        for s in range(S):
+            tt(T.pq[:, s, :], Q[s], T.land2[:, 1, :], mult)
+        V.wait_ge(sem.sq, 1)
+        for s in range(S):
+            tt(ps[:, 8 + s, :], Q[s], T.b2[:], mult)
+        V.wait_ge(sem.ae0, count(0))
+        V.wait_ge(sem.al0, count(0))
+        tt(T.b0[:], T.le0[:], T.ll0[:], add)
         step()
         tt(T.m[:, :, :], ps[:, 8:8 + S, :], w[:, 0:S, :], add)
         step()
         M = T.m
-        Q = [T.pq[:, s, :] for s in range(S)]
-        top -= 1
 
-    V.wait_ge(sem.arr0, count(via[(0, rank)]))
-    if top == 0:
+    if rank == 1:
+        V.wait_ge(sem.arr0, count(0))
         h = S // 2
         for s in range(S):
-            tt(ps[:, 8 + s, :], Q[s], T.land0[:], mult, own=sem.f1 if s < h else sem.f2)
-        V.wait_ge(sem.f1, h)
-        nf2 = S - h
+            tt(ps[:, 8 + s, :], Q[s], T.land0[:, 0, :], mult, own=sem.f1 if s < h else sem.f2)
+        nf1, nf2 = h, S - h
+    elif rank == 2:
+        V.wait_ge(sem.arr0, count(1))
+        V.tensor_copy(T.land0[:, 1, :], T.land0[:, 0, :]).then_inc(sem.sz, 1)
+        tt(ps[:, 8, :], T.pq[:, 0, :], T.land0[:, 0, :], mult, own=sem.f1)
+        tt(ps[:, 9, :], T.pq[:, 1, :], T.land0[:, 0, :], mult, own=sem.f1)
+        V.wait_ge(sem.sz, 1)
+        tt(ps[:, 10:12, :], T.pq[:, 2:4, :], T.land0[:, :, :], mult, own=sem.f1)
+        tt(ps[:, 12:14, :], T.pq[:, 4:6, :], T.land0[:, :, :], mult, own=sem.f2)
+        h, nf1, nf2 = 4, 3, 1
     else:
-        V.wait_ge(sem.arr1, count(via[(1, rank)]))
-        tt(T.hb[:, 0, :], T.land0[:], T.land1[:, 0, :], add, own=sem.sz)
-        tt(T.hb[:, 1, :], T.land0[:], T.land1[:, 0, :], add, own=sem.sz)
-        V.wait_ge(sem.sz, 2)
+        V.wait_ge(sem.arra, count(0))
+        tt(T.zb[:], T.landa[:], T.b0[:], mult, own=sem.sz)
+        V.wait_ge(sem.arr1, count(2))
+        V.wait_ge(sem.sz, 1)
+        tt(T.hb[:, 0, :], T.zb[:], T.land1[:, 0, :], add, own=sem.sz)
+        tt(T.hb[:, 1, :], T.zb[:], T.land1[:, 0, :], add, own=sem.sz)
+        V.wait_ge(sem.sz, 3)
         h = 4
         for s in range(0, S, 2):
             tt(ps[:, 8 + s:10 + s, :], T.pq[:, s:s + 2, :], T.hb[:, :, :], mult, own=sem.f1 if s < h else sem.f2)
-        V.wait_ge(sem.f1, h // 2)
-        nf2 = (S - h) // 2
+        nf1, nf2 = h // 2, (S - h) // 2
+    V.wait_ge(sem.f1, nf1)
     tt(T.yb[:, 0:h, :], ps[:, 8:8 + h, :], M[:, 0:h, :], add, own=sem.ydone)
     V.wait_ge(sem.f2, nf2)
     tt(T.yb[:, h:S, :], ps[:, 8 + h:8 + S, :], M[:, h:S, :], add, own=sem.ydone)

from concourse.mybir import AluOpType

N, S, B = 4, 6, 32

SCRATCH = {
    "w": ("sbuf", [128, S + 1, B], "float32"),
    "gt": ("sbuf", [128, S, B], "float32"),
    "p": ("sbuf", [128, S, B], "float32"),
    "pr": ("sbuf", [128, 2, B], "float32"),
    "c2b": ("sbuf", [128, B], "float32"),
    "bb": ("sbuf", [128, B], "float32"),
    "lb": ("sbuf", [128, B], "float32"),
    "la": ("sbuf", [128, 2, B], "float32"),
    "ap": ("sbuf", [128, B], "float32"),
    "a1b": ("sbuf", [128, B], "float32"),
    "b0": ("sbuf", [128, B], "float32"),
    "b2": ("sbuf", [128, B], "float32"),
    "m": ("sbuf", [128, S, B], "float32"),
    "hb": ("sbuf", [128, 2, B], "float32"),
    "zb": ("sbuf", [128, B], "float32"),
    "yb": ("sbuf", [128, S, B], "float32"),
    "land0": ("sbuf", [128, 2, B], "float32"),
    "landa": ("sbuf", [128, B], "float32"),
    "land1": ("sbuf", [128, 2, B], "float32"),
    "land2": ("sbuf", [128, 2, B], "float32"),
    "lg0": ("sbuf", [128, B], "float32"),
    "le0": ("sbuf", [128, B], "float32"),
    "ll0": ("sbuf", [128, B], "float32"),
    "le2": ("sbuf", [128, B], "float32"),
    "ps": ("psum", [128, 16, B], "float32"),
    "pq": ("psum", [128, S, B], "float32"),
}
SEMAPHORES = ["xl", "gl", "vs", "ready", "ydone", "stored", "sent", "es", "arr0", "arr1", "arr2", "arra", "arrp",
              "ag0", "ae0", "al0", "ae2", "sa1", "st3", "sa2", "sb1", "saa", "spr", "sp1", "sss", "f1", "f2", "sz",
              "sc2", "sl1", "lrdy", "sap", "sq"]


def _routes(cores, topo):
    n = len(cores)

    def ok(a, b):
        return topo.may_write(cores[a], cores[b])

    way = {}
    for j in range(n):
        for r in range(j + 1, n):
            if not ok(j, r):
                c = [k for k in range(n) if k not in (j, r) and ok(j, k) and ok(k, r)]
                way[(j, r)] = [k for k in c if j < k < r] + [k for k in c if not j < k < r]
    return way


def _bits(mask):
    return bin(mask).count("1")


def rank_program(g, core, T, topo):
    rank = T.rank_of(core)
    if rank is None:
        return
    cores = list(T.cores)
    n = len(cores)
    way = _routes(cores, topo)
    assert sorted(way) == [(0, 2), (1, 3)] and way[(0, 2)][0] == 1 and way[(1, 3)] == [2, 0]
    V = g.vector
    sem = T.sem
    mult, add = AluOpType.mult, AluOpType.add
    w, gt, p, ps, pr = T.w, T.gt, T.p, T.ps, T.pr
    first = rank == 0
    raw5 = rank in (0, 2)
    A = T.la[:, 1, :] if rank == 2 else w[:, S, :]

    if first:
        g.sync.dma_start(gt[:, 1:S, :], T.gate[:, B:S * B]).then_inc(sem.gl, 16)
    else:
        g.sync.dma_start(gt[:, :, :], T.gate[:, :]).then_inc(sem.gl, 16)
    g.scalar.dma_start(w[:, 0:S, :], T.x[:, :]).then_inc(sem.xl, 16)

    cnt = {"n": 0, "w": 0}

    def tt(out, a, b, op, own=None):
        ins = V.tensor_tensor(out, a, b, op)
        if own is None:
            ins.then_inc(sem.vs, 1)
            cnt["n"] += 1
        else:
            ins.then_inc(own, 1)

    def step():
        if cnt["n"] > cnt["w"]:
            V.wait_ge(sem.vs, cnt["n"])
            cnt["w"] = cnt["n"]

    lo = 3 if first else 1
    V.wait_ge(sem.gl, 16)
    tt(p[:, lo:S:2, :], gt[:, lo:S:2, :], gt[:, lo - 1:S - 1:2, :], mult, own=sem.sa1)
    V.wait_ge(sem.xl, 16)
    tt(ps[:, 0:3, :], gt[:, 1:S:2, :], w[:, 0:S - 1:2, :], mult, own=sem.st3)
    V.wait_ge(sem.sa1, 1)
    tt(p[:, 4, :], p[:, 5, :], p[:, 3, :], mult, own=sem.sa2)
    V.wait_ge(sem.st3, 1)
    if raw5:
        tt(w[:, 1:4:2, :], ps[:, 0:2, :], w[:, 1:4:2, :], add, own=sem.sb1)
    else:
        tt(w[:, 1:S:2, :], ps[:, 0:3, :], w[:, 1:S:2, :], add, own=sem.sb1)
    V.wait_ge(sem.sa2, 1)
    if first:
        tt(T.c2b[:], ps[:, 2, :], w[:, 5, :], add, own=sem.sc2)
    else:
        tt(A, p[:, 4, :], p[:, 1, :], mult, own=sem.saa)
    V.wait_ge(sem.sb1, 1)
    tt(pr[:, 1, :], p[:, 5, :], w[:, 3, :], mult, own=sem.spr)
    tt(pr[:, 0, :], p[:, 4, :], w[:, 1, :], mult, own=sem.sp1)
    V.wait_ge(sem.spr, 1)
    if first:
        V.wait_ge(sem.sc2, 1)
        tt(ps[:, 3, :], pr[:, 1, :], T.c2b[:], add, own=sem.sss)
        tt(ps[:, 7, :], pr[:, 1, :], ps[:, 2, :], add, own=sem.sl1)
        V.wait_ge(sem.sss, 1)
        V.wait_ge(sem.sp1, 1)
        tt(T.bb[:], ps[:, 3, :], pr[:, 0, :], add, own=sem.ready)
        V.wait_ge(sem.sl1, 1)
        tt(T.lb[:], ps[:, 7, :], pr[:, 0, :], add, own=sem.lrdy)
    elif rank == 2:
        tt(ps[:, 3, :], pr[:, 1, :], ps[:, 2, :], add, own=sem.sss)
        V.wait_ge(sem.sss, 1)
        V.wait_ge(sem.sp1, 1)
        V.wait_ge(sem.saa, 1)
        tt(T.la[:, 0, :], ps[:, 3, :], pr[:, 0, :], add, own=sem.ready)
    else:
        tt(ps[:, 3, :], pr[:, 1, :], w[:, 5, :], add, own=sem.sss)
        if rank == 1:
            tt(T.ap[:], p[:, 4, :], gt[:, 1, :], mult, own=sem.sap)
        V.wait_ge(sem.sss, 1)
        V.wait_ge(sem.sp1, 1)
        V.wait_ge(sem.saa, 1)
        tt(w[:, 5, :], ps[:, 3, :], pr[:, 0, :], add, own=sem.ready)
        if rank == 1:
            V.wait_ge(sem.sap, 1)

    sent = [0]

    def write(dst_rank, out, src, rsem, lsem=None):
        d = cores[dst_rank]
        rid, pid = topo.addr(d, core)
        mk = topo.mask(core, d)
        g.remote_dma(out_ap=out, in_ap=src, remote_sem=rsem, local_sem=sem.sent if lsem is None else lsem, pid=pid,
                     routing_id=rid, dma_engine_mask=mk)
        if lsem is None:
            sent[0] += _bits(mk)
        return _bits(mk)

    def count(src_rank):
        return _bits(topo.mask(cores[src_rank], core))

    left5 = 0
    if rank == 0:
        g.wait_ge(sem.xl, 16)
        write(3, T.le0[:], w[:, 5, :], sem.ae0)
        g.wait_ge(sem.ready, 1)
        write(1, T.land0[:, 0, :], T.bb[:], sem.arr0)
        g.wait_ge(sem.lrdy, 1)
        write(3, T.ll0[:], T.lb[:], sem.al0)
        g.wait_ge(sem.arra, count(1))
        write(3, T.landa[:], T.landa[:], sem.arra)
    elif rank == 1:
        g.wait_ge(sem.gl, 16)
        write(2, T.lg0[:], gt[:, 0, :], sem.ag0)
        g.wait_ge(sem.saa, 1)
        write(0, T.landa[:], w[:, S, :], sem.arra)
        g.wait_ge(sem.ready, 1)
        write(2, T.land1[:, 0, :], w[:, 5, :], sem.arr1)
        g.wait_ge(sem.sap, 1)
        write(2, T.land1[:, 1, :], T.ap[:], sem.arrp)
        g.wait_ge(sem.arr0, count(0))
        write(2, T.land0[:, 0, :], T.land0[:, 0, :], sem.arr0)
    elif rank == 2:
        g.wait_ge(sem.xl, 16)
        left5 = write(3, T.le2[:], w[:, 5, :], sem.ae2, lsem=sem.es)
        g.wait_ge(sem.ready, 1)
        write(3, T.land2[:, :, :], T.la[:, :, :], sem.arr2)
        g.wait_ge(sem.arr1, count(1))
        write(3, T.land1[:, 0, :], T.land1[:, 0, :], sem.arr1)
    if sent[0]:
        g.wait_ge(sem.sent, sent[0])

    tt(ps[:, 4, :], p[:, 3, :], w[:, 1, :], mult)
    step()
    tt(w[:, 3, :], ps[:, 4, :], w[:, 3, :], add)
    if not first:
        tt(p[:, 3, :], p[:, 3, :], p[:, 1, :], mult)
    step()
    tt(ps[:, 5:7, :], gt[:, 2:S - 1:2, :], w[:, 1:S - 2:2, :], mult)
    if not first:
        tt(p[:, 2:S - 1:2, :], gt[:, 2:S - 1:2, :], p[:, 1:S - 2:2, :], mult)
    step()
    tt(w[:, 2:S - 1:2, :], ps[:, 5:7, :], w[:, 2:S - 1:2, :], add)
    V.wait_ge(sem.ready, 1)
    if rank == 2:
        V.wait_ge(sem.es, left5)
        tt(w[:, 5, :], T.la[:, 0, :], w[:, 5, :], add)
    step()
    if first:
        g.sync.wait_ge(sem.vs, cnt["n"])
        g.sync.wait_ge(sem.ready, 1)
        g.sync.dma_start(T.y[:, 0:(S - 1) * B], w[:, 0:S - 1, :]).then_inc(sem.stored, 16)
        g.sync.dma_start(T.y[:, (S - 1) * B:S * B], T.bb[:]).then_inc(sem.stored, 16)
        g.sync.wait_ge(sem.stored, 32)
        return

    M = w
    Q = [gt[:, 0, :]] + [p[:, s, :] for s in range(1, S - 1)] + [A]
    if rank == 2:
        V.wait_ge(sem.arr1, count(1))
        for s in range(S):
            tt(ps[:, 8 + s, :], Q[s], T.land1[:, 0, :], mult)
        V.wait_ge(sem.ag0, count(1))
        V.wait_ge(sem.arrp, count(1))
        tt(T.a1b[:], T.lg0[:], T.land1[:, 1, :], mult, own=sem.sq)
        step()
        tt(T.m[:, :, :], ps[:, 8:8 + S, :], w[:, 0:S, :], add)
        V.wait_ge(sem.sq, 1)
        for s in range(S):
            tt(T.pq[:, s, :], Q[s], T.a1b[:], mult)
        step()
        M = T.m
    elif rank == 3:
        V.wait_ge(sem.ae2, count(2))
        V.wait_ge(sem.arr2, count(2))
        tt(T.b2[:], T.le2[:], T.land2[:, 0, :], add, own=sem.sq)
        for s in range(S):
            tt(T.pq[:, s, :], Q[s], T.land2[:, 1, :], mult)
        V.wait_ge(sem.sq, 1)
        for s in range(S):
            tt(ps[:, 8 + s, :], Q[s], T.b2[:], mult)
        V.wait_ge(sem.ae0, count(0))
        V.wait_ge(sem.al0, count(0))
        tt(T.b0[:], T.le0[:], T.ll0[:], add)
        step()
        tt(T.m[:, :, :], ps[:, 8:8 + S, :], w[:, 0:S, :], add)
        step()
        M = T.m

    if rank == 1:
        V.wait_ge(sem.arr0, count(0))
        h = S // 2
        for s in range(S):
            tt(ps[:, 8 + s, :], Q[s], T.land0[:, 0, :], mult, own=sem.f1 if s < h else sem.f2)
        nf1, nf2 = h, S - h
    elif rank == 2:
        V.wait_ge(sem.arr0, count(1))
        V.tensor_copy(T.land0[:, 1, :], T.land0[:, 0, :]).then_inc(sem.sz, 1)
        tt(ps[:, 8, :], T.pq[:, 0, :], T.land0[:, 0, :], mult, own=sem.f1)
        tt(ps[:, 9, :], T.pq[:, 1, :], T.land0[:, 0, :], mult, own=sem.f1)
        V.wait_ge(sem.sz, 1)
        tt(ps[:, 10:12, :], T.pq[:, 2:4, :], T.land0[:, :, :], mult, own=sem.f1)
        tt(ps[:, 12:14, :], T.pq[:, 4:6, :], T.land0[:, :, :], mult, own=sem.f2)
        h, nf1, nf2 = 4, 3, 1
    else:
        V.wait_ge(sem.arra, count(0))
        tt(T.zb[:], T.landa[:], T.b0[:], mult, own=sem.sz)
        V.wait_ge(sem.arr1, count(2))
        V.wait_ge(sem.sz, 1)
        tt(T.hb[:, 0, :], T.zb[:], T.land1[:, 0, :], add, own=sem.sz)
        tt(T.hb[:, 1, :], T.zb[:], T.land1[:, 0, :], add, own=sem.sz)
        V.wait_ge(sem.sz, 3)
        h = 4
        for s in range(0, S, 2):
            tt(ps[:, 8 + s:10 + s, :], T.pq[:, s:s + 2, :], T.hb[:, :, :], mult, own=sem.f1 if s < h else sem.f2)
        nf1, nf2 = h // 2, (S - h) // 2
    V.wait_ge(sem.f1, nf1)
    tt(T.yb[:, 0:h, :], ps[:, 8:8 + h, :], M[:, 0:h, :], add, own=sem.ydone)
    V.wait_ge(sem.f2, nf2)
    tt(T.yb[:, h:S, :], ps[:, 8 + h:8 + S, :], M[:, h:S, :], add, own=sem.ydone)
    g.sync.wait_ge(sem.ydone, 2)
    g.sync.dma_start(T.y[:, :], T.yb[:, :, :]).then_inc(sem.stored, 16)
    g.sync.wait_ge(sem.stored, 16)
